import numpy as np
import ml_dtypes


def mxq(x, axis, fmt="e4m3"):
    dtype, down = {"e4m3": (ml_dtypes.float8_e4m3fn, 7), "e5m2": (ml_dtypes.float8_e5m2, 14)}[fmt]
    v = np.moveaxis(np.asarray(x, np.float32).astype(ml_dtypes.bfloat16).astype(np.float64), axis, -1)
    blocks = v.reshape(v.shape[:-1] + (-1, 32))
    amax = np.abs(blocks).max(-1, keepdims=True)
    byte = np.maximum(np.where(amax > 0, np.frexp(amax)[1] - 1 + 127, 0) - down, 1)
    scale = np.exp2(byte - 127.0)
    codes = (blocks / scale).astype(np.float32).astype(dtype).astype(np.float64)
    return np.moveaxis((codes * scale).reshape(v.shape), -1, axis)


WIDE = False


def mx_kscale(k):
    if not WIDE:
        return np.ones(k)
    levels = np.array([10, -10, 5, -5, 0])
    if k % 512:
        return np.exp2(np.random.permutation(np.resize(levels, k // 32))).repeat(32)
    a = np.empty((k // 512, 16))
    for p in range(k // 512):
        a[p, :8] = np.random.permutation(np.resize(levels, 8))
        for g in range(8):
            far = levels[np.abs(levels - a[p, g]) >= 10]
            a[p, g + 8] = far[np.random.randint(len(far))]
    return np.exp2(a.ravel()).repeat(32)


def f64(x):
    return np.asarray(x).astype(np.float64)


def striped(idx):
    return np.tile(idx.reshape(-1, 16).T, (8, 1)).astype(np.uint16)


def unstriped(offs):
    return offs[:16].T.reshape(-1).astype(np.int64)


def striped8(idx):
    return np.concatenate([x.reshape(-1, 16).T for x in idx]).astype(np.uint16)


def runs(offs, k):
    lists = np.stack([offs[16 * r : 16 * r + 16].T.reshape(-1) for r in range(8)]).astype(np.int64)
    return lists[np.arange(k) % 512 // 64]


def pack_weight(w):
    k, n = w.shape
    w = f64(np.asarray(w, np.float32).astype(ml_dtypes.bfloat16)).reshape(k // 32, 32, n)
    amax = np.abs(w).max(1)
    byte = np.clip(np.where(amax > 0, np.frexp(amax)[1] - 1 + 127 - 7, 1), 1, 254)
    scaled = (w * np.exp2(127.0 - byte)[:, None, :]).reshape(k, n).astype(np.float32)
    words = np.ascontiguousarray(scaled.reshape(k // 512, 128, 4, n).transpose(0, 1, 3, 2)).astype(ml_dtypes.float8_e4m3fn).view(np.uint8)
    return words, np.ascontiguousarray(byte.astype(np.uint8).reshape(k // 512, 16, n))


def unpack_weight(words, scales):
    g, p, n, _ = words.shape
    vals = np.ascontiguousarray(words).view(ml_dtypes.float8_e4m3fn).astype(np.float64) * np.repeat(np.exp2(scales.astype(np.float64) - 127.0), 8, axis=1)[..., None]
    return vals.transpose(0, 1, 3, 2).reshape(g * 512, n)


def sigmoid(v):
    return 1.0 / (1.0 + np.exp(-np.maximum(v, -700.0)))


K, T, S, N, H, W = 512, 2048, 512, 512, 512, 256


def setup_inputs():
    n = np.random.standard_normal
    s = mx_kscale(K)[:, None]
    u = mx_kscale(H)
    packed_xT = pack_weight(n((K, T)) * s)
    perm = np.random.permutation(S)
    return {
        "x_words": packed_xT[0],
        "x_scales": packed_xT[1],
        "w1": (n((K, H)) / np.sqrt(K) / s).astype(np.float32),
        "sl": np.random.uniform(1.0, 2.0, (H, 1)).astype(np.float32),
        "th": (0.5 * n((H, 1))).astype(np.float32),
        "gn": (np.random.uniform(0.5, 1.5, (H, 1)) * u[:, None]).astype(np.float32),
        "w2": (n((H, N)) / np.sqrt(H) / u[:, None]).astype(np.float32),
        "offs": striped8(np.random.randint(0, T, (8, S))),
        "n1": striped(np.random.permutation(S)),
        "n2": striped(np.random.permutation(S)),
        "n3": striped(perm[:W]),
        "n4": striped(perm[W:]),
    }


def reference(x_words, x_scales, w1, sl, th, gn, w2, offs, n1, n2, n3, n4):
    xq = unpack_weight(x_words, x_scales)[np.arange(K)[:, None], runs(offs, K)]
    y = mxq(f64(w1), 0, "e4m3").T @ xq
    ds = np.zeros((H, S))
    ds[:, unstriped(n1)] = y
    sg = sigmoid(f64(sl) * (ds[:, unstriped(n2)] - f64(th)))
    z = f64(gn) * (y * sg)
    h = mxq(f64(w2), 0, "e4m3").T @ mxq(z, 0, "e4m3")
    pa = h[:, unstriped(n3)]
    pb = h[:, unstriped(n4)]
    rb = np.maximum(pa, pb)
    ra = pa / (np.abs(pb) + 0.5)
    ds2 = np.zeros((N, S))
    ds2[:, unstriped(n3)] = ra
    out = ds2.copy()
    out[:, unstriped(n4)] = rb
    return out

@@ -1,0 +1,286 @@
+from contextlib import ExitStack
+
+import concourse.mybir as mybir
+
+K, T, S, N, H, W = 512, 2048, 512, 512, 512, 256
+FLOPS = 2 * K * H * S + 2 * H * N * S
+
+F32 = mybir.dt.float32
+BF16 = mybir.dt.bfloat16
+I32 = mybir.dt.int32
+U32 = mybir.dt.uint32
+U16 = mybir.dt.uint16
+U8 = mybir.dt.uint8
+FP8X4 = mybir.dt.float8_e4m3fn_x4
+ALU = mybir.AluOpType
+ACT = mybir.ActivationFunctionType
+
+P = 128
+PACK = 4
+HALF = S // 2
+LIST_COLS = HALF // 16
+
+
+def tile_picked_hasherlratio_none_p_kernel(
+    tc, x_words, x_scales, w1, sl, th, gn, w2, offs, n1, n2, n3, n4, out
+):
+    nc = tc.nc
+    with ExitStack() as ctx:
+        lists = ctx.enter_context(tc.tile_pool(name="lists", bufs=1))
+        sb = ctx.enter_context(tc.tile_pool(name="sb", bufs=1))
+        psum = ctx.enter_context(tc.psum_pool(name="psum", bufs=1))
+
+        def tile(shape, dtype, name, tag=None):
+            return sb.tile(shape, dtype, name=name, tag=tag or name, align_bytes=64)
+
+        def load_list(src, name):
+            t = lists.tile(list(src.shape), U16, name=name)
+            nc.sync.dma_start(t[:], src)
+            return t
+
+        def half_of(lst, a):
+            return lst[:, a * LIST_COLS : (a + 1) * LIST_COLS]
+
+        def cols(a):
+            return slice(a * HALF, (a + 1) * HALF)
+
+        scale_table = tile([P, T], U8, "scale_table")
+        offs_sb = load_list(offs, "offs_sb")
+        scale_rows = x_scales[0].bitcast(I32).unsqueeze(1).to_broadcast([16, 8, T // 4])
+        nc.sync.dma_start(scale_table[:].bitcast(I32), scale_rows)
+        w1_rows = w1.rearrange("(p j) c -> p j c", j=PACK)
+        w1_raw = []
+        for c in range(2):
+            w1_raw.append(tile([P, PACK, H // 2], F32, "w1_raw%d" % c, tag="w_raw%d" % c))
+            nc.sync.dma_start(w1_raw[c][:], w1_rows[:, :, c * (H // 2) : (c + 1) * (H // 2)])
+        word_table = tile([P, T], U32, "word_table")
+        nc.sync.dma_start(word_table[:].bitcast(I32), x_words[0].rearrange("p c r -> p (c r)").bitcast(I32))
+        n1_sb = load_list(n1, "n1_sb")
+        n2_sb = load_list(n2, "n2_sb")
+        n3_sb = load_list(n3, "n3_sb")
+        n4_sb = load_list(n4, "n4_sb")
+        row_vals = {}
+        for name, src in (("sl", sl), ("th", th), ("gn", gn)):
+            row_vals[name] = tile([P, PACK], F32, name + "_sb")
+            nc.gpsimd.dma_start(row_vals[name][:], src.rearrange("(p t) o -> p (t o)", t=PACK))
+        sl_sb, th_sb, gn_sb = row_vals["sl"], row_vals["th"], row_vals["gn"]
+
+        picked_scales = tile([P, S], U8, "picked_scales")
+        nc.vector.tensor_copy(picked_scales[:], scale_table[:].indirect(offs_sb[:]))
+        x_scale = tile([P, S], U8, "x_scale")
+        nc.vector.tensor_copy(x_scale[:].bitcast(I32), picked_scales[:].bitcast(I32))
+        for r in range(1, 4):
+            nc.scalar.dma_start(
+                x_scale[:].bitcast(I32)[r:P:32, :], picked_scales[:].bitcast(I32)[8 * r : P : 32, :]
+            )
+
+        w1_bf = tile([P, PACK, P, PACK], BF16, "w1_bf")
+        w1_dst = w1_bf[:].rearrange("p t m j -> p m t j")
+        for c in range(2):
+            nc.vector.tensor_copy(
+                w1_dst[:, c * (P // 2) : (c + 1) * (P // 2)], w1_raw[c][:].rearrange("p j (m t) -> p m t j", t=PACK)
+            )
+        w1_codes = tile([P, H], U32, "w1_codes")
+        w1_scale = tile([P, H], U8, "w1_scale")
+        nc.vector.quantize_mx(
+            out=w1_codes[:].bitcast(FP8X4), scales=w1_scale[:], in_=w1_bf[:].rearrange("p t m j -> p (t m j)")
+        )
+
+        w2_rows = w2.rearrange("(p j) c -> p j c", j=PACK)
+        w2_raw = []
+        for c in range(2):
+            w2_raw.append(tile([P, PACK, N // 2], F32, "w2_raw%d" % c, tag="w_raw%d" % c))
+            nc.sync.dma_start(w2_raw[c][:], w2_rows[:, :, c * (N // 2) : (c + 1) * (N // 2)])
+
+        y_ps = {}
+        for a in range(2):
+            picked_words = tile([P, HALF], U32, "picked_words%d" % a)
+            nc.vector.tensor_copy(picked_words[:], word_table[:].indirect(half_of(offs_sb, a)))
+            for t in range(PACK):
+                y_ps[t, a] = psum.tile([P, HALF], F32, name="y_ps%d_%d" % (t, a), tag="bank%d" % (4 * a + t))
+                nc.tensor.matmul_mx(
+                    out=y_ps[t, a][:],
+                    lhsT=w1_codes[:, t * P : (t + 1) * P].bitcast(FP8X4),
+                    lhsT_scale=w1_scale[:, t * P : (t + 1) * P],
+                    rhs=picked_words[:].bitcast(FP8X4),
+                    rhs_scale=x_scale[:, cols(a)],
+                    start=True,
+                    stop=True,
+                )
+
+        sig_bias = tile([P, PACK], F32, "sig_bias")
+        nc.vector.scalar_tensor_tensor(sig_bias[:], sl_sb[:], -1.0, th_sb[:], ALU.mult, ALU.mult)
+        y_sb = {}
+        ds = [tile([P, S], F32, "ds%d" % t) for t in range(PACK)]
+        sg = {}
+        z_planes = [tile([P, PACK, HALF], BF16, "z_planes%d" % a) for a in range(2)]
+
+        def y_out(t, a):
+            name = "y_sb%d_%d" % (t, a)
+            y_sb[t, a] = tile([P, HALF], F32, name, tag="rounded0" if (t, a) == (3, 1) else name)
+            nc.scalar.copy(y_sb[t, a][:], y_ps[t, a][:])
+
+        def y_scatter(t, a):
+            target = ds[t][:].indirect(half_of(n1_sb, a))
+            if t % 2 == 0 or (t, a) == (3, 1):
+                nc.vector.tensor_copy(target, y_sb[t, a][:])
+            else:
+                nc.scalar.activation(target, y_sb[t, a][:], ACT.Copy)
+
+        def gate(t, a):
+            sg[t, a] = tile([P, HALF], F32, "sg%d_%d" % (t, a))
+            nc.scalar.activation(
+                sg[t, a][:],
+                ds[t][:].indirect(half_of(n2_sb, a)),
+                ACT.Sigmoid,
+                bias=sig_bias[:, t : t + 1],
+                scale=sl_sb[:, t : t + 1],
+            )
+
+        def z_plane(t, a):
+            nc.vector.scalar_tensor_tensor(
+                z_planes[a][:, t, :], y_ps[t, a][:], gn_sb[:, t : t + 1], sg[t, a][:], ALU.mult, ALU.mult
+            )
+
+        w2_bf = {}
+        w2_codes = [tile([P, N // 2], U32, "w2_codes%d" % c) for c in range(2)]
+        w2_scale = [tile([P, N // 2], U8, "w2_scale%d" % c) for c in range(2)]
+
+        def w2_round(c):
+            src = w2_raw[c][:]
+            w2_bf[c] = tile([P, N // 2, PACK], BF16, "w2_bf%d" % c, tag="rounded%d" % c)
+            nc.vector.tensor_copy(
+                w2_bf[c][:].rearrange("p (c i) j -> p c j i", i=4), src.rearrange("p j (c i) -> p c j i", i=4)
+            )
+
+        def w2_quantize(c):
+            nc.vector.quantize_mx(
+                out=w2_codes[c][:].bitcast(FP8X4), scales=w2_scale[c][:], in_=w2_bf[c][:].rearrange("p c j -> p (c j)")
+            )
+
+        h_ps = {}
+
+        z_codes, z_scale = {}, {}
+
+        def z_quantize(a):
+            z_bf = tile([P, HALF, PACK], BF16, "z_bf%d" % a, tag="rounded%d" % (2 - a))
+            nc.vector.tensor_copy(
+                z_bf[:].rearrange("p (c i) t -> p c t i", i=4), z_planes[a][:].rearrange("p t (c i) -> p c t i", i=4)
+            )
+            z_codes[a] = tile([P, HALF], U32, "z_codes%d" % a)
+            z_scale[a] = tile([P, HALF], U8, "z_scale%d" % a)
+            nc.vector.quantize_mx(
+                out=z_codes[a][:].bitcast(FP8X4), scales=z_scale[a][:], in_=z_bf[:].rearrange("p c t -> p (c t)")
+            )
+
+        def second_product(a, row_tiles):
+            for m in row_tiles:
+                mc = slice((m % 2) * P, (m % 2 + 1) * P)
+                h_ps[m, a] = psum.tile([P, HALF], F32, name="h_ps%d_%d" % (m, a), tag="bank%d" % (4 * a + m))
+                nc.tensor.matmul_mx(
+                    out=h_ps[m, a][:],
+                    lhsT=w2_codes[m // 2][:, mc].bitcast(FP8X4),
+                    lhsT_scale=w2_scale[m // 2][:, mc],
+                    rhs=z_codes[a][:].bitcast(FP8X4),
+                    rhs_scale=z_scale[a][:],
+                    start=True,
+                    stop=True,
+                )
+
+        for t in range(PACK):
+            y_out(t, 0)
+        y_out(0, 1)
+        y_out(2, 1)
+        y_scatter(0, 0)
+        y_scatter(3, 0)
+        y_out(1, 1)
+        y_scatter(2, 0)
+        y_scatter(1, 0)
+        y_scatter(0, 1)
+        y_out(3, 1)
+        y_scatter(1, 1)
+        y_scatter(2, 1)
+        y_scatter(3, 1)
+        w2_round(0)
+        w2_quantize(0)
+        for a in range(2):
+            for t in range(PACK):
+                gate(t, a)
+        for a in range(2):
+            for t in range(PACK):
+                z_plane(t, a)
+            z_quantize(a)
+            second_product(a, (0, 1))
+        w2_round(1)
+        w2_quantize(1)
+        for a in range(2):
+            second_product(a, (2, 3))
+
+        pa, pb, rb, inv = {}, {}, {}, {}
+        res = [tile([P, S], F32, "res%d" % m) for m in range(PACK)]
+
+        h_all = [tile([P, S], F32, "h_sb%d" % m) for m in range(PACK)]
+
+        def h_out(m, a):
+            if m == 2:
+                nc.vector.tensor_copy(h_all[m][:, cols(a)], h_ps[m, a][:])
+            else:
+                nc.scalar.copy(h_all[m][:, cols(a)], h_ps[m, a][:])
+
+        size, root = {}, {}
+
+        def fetch(m):
+            pb[m] = tile([P, W], F32, "pb%d" % m)
+            pa[m] = tile([P, W], F32, "pa%d" % m)
+            for dst, lst in ((pb[m], n4_sb), (pa[m], n3_sb)):
+                if m == 1:
+                    nc.scalar.activation(dst[:], h_all[m][:].indirect(lst[:]), ACT.Copy)
+                else:
+                    nc.vector.tensor_copy(dst[:], h_all[m][:].indirect(lst[:]))
+
+        def larger(m):
+            rb[m] = tile([P, W], F32, "rb%d" % m)
+            nc.vector.tensor_tensor(rb[m][:], pa[m][:], pb[m][:], ALU.max)
+
+        def magnitude(m):
+            size[m] = tile([P, W], F32, "size%d" % m)
+            nc.scalar.activation(size[m][:], pb[m][:], ACT.Abs)
+
+        def inverse_root(m):
+            root[m] = tile([P, W], F32, "root%d" % m)
+            nc.scalar.activation(root[m][:], size[m][:], ACT.Abs_reciprocal_sqrt, bias=0.5)
+
+        def inverse(m):
+            inv[m] = tile([P, W], F32, "inv%d" % m)
+            nc.scalar.activation(inv[m][:], root[m][:], ACT.Square)
+
+        def put_ratio(m):
+            nc.vector.tensor_tensor(res[m][:].indirect(n3_sb[:]), pa[m][:], inv[m][:], ALU.mult)
+
+        def put_larger(m):
+            nc.scalar.activation(res[m][:].indirect(n4_sb[:]), rb[m][:], ACT.Copy)
+
+        def store(m):
+            nc.sync.dma_start(out[m * P : (m + 1) * P, :], res[m][:])
+
+        def prepare(pair):
+            for step in (fetch, larger, magnitude, inverse_root, inverse):
+                for m in pair:
+                    step(m)
+
+        for a in range(2):
+            h_out(0, a)
+            h_out(1, a)
+        prepare((0, 1))
+        for m in (2, 3):
+            for a in range(2):
+                h_out(m, a)
+        put_larger(1)
+        prepare((2, 3))
+        for m in range(PACK):
+            if m > 0:
+                put_larger((m + 1) % PACK)
+            put_ratio(m)
+            if m > 0:
+                store(m)
+        store(0)

@@ -65,6 +65,8 @@ def tile_picked_hasherlratio_none_p_kernel(
             nc.gpsimd.dma_start(row_vals[name][:], src.rearrange("(p t) o -> p (t o)", t=PACK))
         sl_sb, th_sb, gn_sb = row_vals["sl"], row_vals["th"], row_vals["gn"]
 
+        warm_sigmoid = tile([P, 1], F32, "warm_sigmoid")
+        nc.scalar.activation(warm_sigmoid[:], sl_sb[:, 0:1], ACT.Sigmoid)
         picked_scales = tile([P, S], U8, "picked_scales")
         nc.vector.tensor_copy(picked_scales[:], scale_table[:].indirect(offs_sb[:]))
         x_scale = tile([P, S], U8, "x_scale")
@@ -206,6 +208,8 @@ def tile_picked_hasherlratio_none_p_kernel(
         for a in range(2):
             for t in range(PACK):
                 gate(t, a)
+        warm_root = tile([P, 1], F32, "warm_root")
+        nc.scalar.activation(warm_root[:], sg[3, 1][:, 0:1], ACT.Abs_reciprocal_sqrt, bias=0.5)
         for a in range(2):
             for t in range(PACK):
                 z_plane(t, a)

@@ -19,6 +19,10 @@ P = 128
 PACK = 4
 HALF = S // 2
 LIST_COLS = HALF // 16
+GATES = ((0, 0), (1, 0), (2, 0), (0, 1), (3, 0), (1, 1), (2, 1), (3, 1))
+SC_FETCH = ()
+VEC_H = ()
+VEC_OUT = ()
 
 
 def tile_picked_hasherlratio_none_p_kernel(
@@ -44,15 +48,15 @@ def tile_picked_hasherlratio_none_p_kernel(
         def cols(a):
             return slice(a * HALF, (a + 1) * HALF)
 
+        def gpsimd_copy(dst, src):
+            nc.gpsimd.tensor_scalar(dst, src, 1.0, 0.0, ALU.mult, ALU.add)
+
         scale_table = tile([P, T], U8, "scale_table")
         offs_sb = load_list(offs, "offs_sb")
         scale_rows = x_scales[0].bitcast(I32).unsqueeze(1).to_broadcast([16, 8, T // 4])
         nc.sync.dma_start(scale_table[:].bitcast(I32), scale_rows)
-        w1_rows = w1.rearrange("(p j) c -> p j c", j=PACK)
-        w1_raw = []
-        for c in range(2):
-            w1_raw.append(tile([P, PACK, H // 2], F32, "w1_raw%d" % c, tag="w_raw%d" % c))
-            nc.sync.dma_start(w1_raw[c][:], w1_rows[:, :, c * (H // 2) : (c + 1) * (H // 2)])
+        w1_raw = tile([P, PACK, H], F32, "w1_raw", tag="w_raw")
+        nc.sync.dma_start(w1_raw[:], w1.rearrange("(p j) c -> p j c", j=PACK))
         word_table = tile([P, T], U32, "word_table")
         nc.sync.dma_start(word_table[:].bitcast(I32), x_words[0].rearrange("p c r -> p (c r)").bitcast(I32))
         n1_sb = load_list(n1, "n1_sb")
@@ -66,33 +70,27 @@ def tile_picked_hasherlratio_none_p_kernel(
         sl_sb, th_sb, gn_sb = row_vals["sl"], row_vals["th"], row_vals["gn"]
 
         warm_sigmoid = tile([P, 1], F32, "warm_sigmoid")
-        nc.scalar.activation(warm_sigmoid[:], sl_sb[:, 0:1], ACT.Sigmoid)
+        nc.scalar.activation(warm_sigmoid[:], w1_raw[:, 0, 0:1], ACT.Sigmoid)
         picked_scales = tile([P, S], U8, "picked_scales")
         nc.vector.tensor_copy(picked_scales[:], scale_table[:].indirect(offs_sb[:]))
         x_scale = tile([P, S], U8, "x_scale")
         nc.vector.tensor_copy(x_scale[:].bitcast(I32), picked_scales[:].bitcast(I32))
         for r in range(1, 4):
-            nc.scalar.dma_start(
+            nc.sync.dma_start(
                 x_scale[:].bitcast(I32)[r:P:32, :], picked_scales[:].bitcast(I32)[8 * r : P : 32, :]
             )
 
         w1_bf = tile([P, PACK, P, PACK], BF16, "w1_bf")
         w1_dst = w1_bf[:].rearrange("p t m j -> p m t j")
-        for c in range(2):
-            nc.vector.tensor_copy(
-                w1_dst[:, c * (P // 2) : (c + 1) * (P // 2)], w1_raw[c][:].rearrange("p j (m t) -> p m t j", t=PACK)
-            )
+        nc.vector.tensor_copy(w1_dst, w1_raw[:].rearrange("p j (m t) -> p m t j", t=PACK))
         w1_codes = tile([P, H], U32, "w1_codes")
         w1_scale = tile([P, H], U8, "w1_scale")
         nc.vector.quantize_mx(
             out=w1_codes[:].bitcast(FP8X4), scales=w1_scale[:], in_=w1_bf[:].rearrange("p t m j -> p (t m j)")
         )
 
-        w2_rows = w2.rearrange("(p j) c -> p j c", j=PACK)
-        w2_raw = []
-        for c in range(2):
-            w2_raw.append(tile([P, PACK, N // 2], F32, "w2_raw%d" % c, tag="w_raw%d" % c))
-            nc.sync.dma_start(w2_raw[c][:], w2_rows[:, :, c * (N // 2) : (c + 1) * (N // 2)])
+        w2_raw = tile([P, PACK, N], F32, "w2_raw", tag="w_raw")
+        nc.sync.dma_start(w2_raw[:], w2.rearrange("(p j) c -> p j c", j=PACK))
 
         y_ps = {}
         for a in range(2):
@@ -111,16 +109,20 @@ def tile_picked_hasherlratio_none_p_kernel(
                 )
 
         sig_bias = tile([P, PACK], F32, "sig_bias")
-        nc.vector.scalar_tensor_tensor(sig_bias[:], sl_sb[:], -1.0, th_sb[:], ALU.mult, ALU.mult)
+        sl_th = tile([P, PACK], F32, "sl_th")
+        nc.gpsimd.tensor_tensor(sl_th[:], sl_sb[:], th_sb[:], ALU.mult)
+        nc.gpsimd.tensor_scalar(sig_bias[:], sl_th[:], -1.0, 0.0, ALU.mult, ALU.add)
         y_sb = {}
         ds = [tile([P, S], F32, "ds%d" % t) for t in range(PACK)]
         sg = {}
-        z_planes = [tile([P, PACK, HALF], BF16, "z_planes%d" % a) for a in range(2)]
+        z_planes = {}
 
         def y_out(t, a):
-            name = "y_sb%d_%d" % (t, a)
-            y_sb[t, a] = tile([P, HALF], F32, name, tag="rounded0" if (t, a) == (3, 1) else name)
-            nc.scalar.copy(y_sb[t, a][:], y_ps[t, a][:])
+            y_sb[t, a] = tile([P, HALF], F32, "y_sb%d_%d" % (t, a))
+            if (t, a) in VEC_OUT:
+                nc.vector.tensor_copy(y_sb[t, a][:], y_ps[t, a][:])
+            else:
+                nc.scalar.copy(y_sb[t, a][:], y_ps[t, a][:])
 
         def y_scatter(t, a):
             target = ds[t][:].indirect(half_of(n1_sb, a))
@@ -140,6 +142,8 @@ def tile_picked_hasherlratio_none_p_kernel(
             )
 
         def z_plane(t, a):
+            if t == 0:
+                z_planes[a] = tile([P, PACK, HALF], BF16, "z_planes%d" % a, tag="planes%d" % a)
             nc.vector.scalar_tensor_tensor(
                 z_planes[a][:, t, :], y_ps[t, a][:], gn_sb[:, t : t + 1], sg[t, a][:], ALU.mult, ALU.mult
             )
@@ -149,11 +153,9 @@ def tile_picked_hasherlratio_none_p_kernel(
         w2_scale = [tile([P, N // 2], U8, "w2_scale%d" % c) for c in range(2)]
 
         def w2_round(c):
-            src = w2_raw[c][:]
-            w2_bf[c] = tile([P, N // 2, PACK], BF16, "w2_bf%d" % c, tag="rounded%d" % c)
-            nc.vector.tensor_copy(
-                w2_bf[c][:].rearrange("p (c i) j -> p c j i", i=4), src.rearrange("p j (c i) -> p c j i", i=4)
-            )
+            src = w2_raw[:, :, c * (N // 2) : (c + 1) * (N // 2)]
+            w2_bf[c] = tile([P, N // 2, PACK], BF16, "w2_bf%d" % c, tag="planes%d" % c)
+            gpsimd_copy(w2_bf[c][:].rearrange("p (c i) j -> p c j i", i=4), src.rearrange("p j (c i) -> p c j i", i=4))
 
         def w2_quantize(c):
             nc.vector.quantize_mx(
@@ -165,7 +167,7 @@ def tile_picked_hasherlratio_none_p_kernel(
         z_codes, z_scale = {}, {}
 
         def z_quantize(a):
-            z_bf = tile([P, HALF, PACK], BF16, "z_bf%d" % a, tag="rounded%d" % (2 - a))
+            z_bf = tile([P, HALF, PACK], BF16, "z_bf%d" % a)
             nc.vector.tensor_copy(
                 z_bf[:].rearrange("p (c i) t -> p c t i", i=4), z_planes[a][:].rearrange("p t (c i) -> p c t i", i=4)
             )
@@ -203,22 +205,19 @@ def tile_picked_hasherlratio_none_p_kernel(
         y_scatter(1, 1)
         y_scatter(2, 1)
         y_scatter(3, 1)
-        w2_round(0)
-        w2_quantize(0)
-        for a in range(2):
-            for t in range(PACK):
-                gate(t, a)
+        for c in range(2):
+            w2_round(c)
+        for c in range(2):
+            w2_quantize(c)
+        for t, a in GATES:
+            gate(t, a)
         warm_root = tile([P, 1], F32, "warm_root")
         nc.scalar.activation(warm_root[:], sg[3, 1][:, 0:1], ACT.Abs_reciprocal_sqrt, bias=0.5)
         for a in range(2):
             for t in range(PACK):
                 z_plane(t, a)
             z_quantize(a)
-            second_product(a, (0, 1))
-        w2_round(1)
-        w2_quantize(1)
-        for a in range(2):
-            second_product(a, (2, 3))
+            second_product(a, range(PACK))
 
         pa, pb, rb, inv = {}, {}, {}, {}
         res = [tile([P, S], F32, "res%d" % m) for m in range(PACK)]
@@ -226,7 +225,7 @@ def tile_picked_hasherlratio_none_p_kernel(
         h_all = [tile([P, S], F32, "h_sb%d" % m) for m in range(PACK)]
 
         def h_out(m, a):
-            if m == 2:
+            if (m, a) in VEC_H:
                 nc.vector.tensor_copy(h_all[m][:, cols(a)], h_ps[m, a][:])
             else:
                 nc.scalar.copy(h_all[m][:, cols(a)], h_ps[m, a][:])
@@ -236,8 +235,8 @@ def tile_picked_hasherlratio_none_p_kernel(
         def fetch(m):
             pb[m] = tile([P, W], F32, "pb%d" % m)
             pa[m] = tile([P, W], F32, "pa%d" % m)
-            for dst, lst in ((pb[m], n4_sb), (pa[m], n3_sb)):
-                if m == 1:
+            for i, (dst, lst) in enumerate(((pb[m], n4_sb), (pa[m], n3_sb))):
+                if (m, i) in SC_FETCH:
                     nc.scalar.activation(dst[:], h_all[m][:].indirect(lst[:]), ACT.Copy)
                 else:
                     nc.vector.tensor_copy(dst[:], h_all[m][:].indirect(lst[:]))
@@ -273,12 +272,9 @@ def tile_picked_hasherlratio_none_p_kernel(
                     step(m)
 
         for a in range(2):
-            h_out(0, a)
-            h_out(1, a)
-        prepare((0, 1))
-        for m in (2, 3):
-            for a in range(2):
+            for m in range(PACK):
                 h_out(m, a)
+        prepare((0, 1))
         put_larger(1)
         prepare((2, 3))
         for m in range(PACK):

@@ -17,12 +17,13 @@ ACT = mybir.ActivationFunctionType
 
 P = 128
 PACK = 4
+TILES = range(PACK)
+HALVES = range(2)
 HALF = S // 2
-LIST_COLS = HALF // 16
-GATES = ((0, 0), (1, 0), (2, 0), (0, 1), (3, 0), (1, 1), (2, 1), (3, 1))
-SC_FETCH = ()
-VEC_H = ()
-VEC_OUT = ()
+GROUP = 16
+BLOCK_ROWS = 8
+QUADRANT = 32
+RUN = 4
 
 
 def tile_picked_hasherlratio_none_p_kernel(
@@ -37,23 +38,49 @@ def tile_picked_hasherlratio_none_p_kernel(
         def tile(shape, dtype, name, tag=None):
             return sb.tile(shape, dtype, name=name, tag=tag or name, align_bytes=64)
 
+        def bank(name, t, half):
+            return psum.tile([P, HALF], F32, name="%s%d_%d" % (name, t, half), tag="bank%d" % (PACK * half + t))
+
         def load_list(src, name):
-            t = lists.tile(list(src.shape), U16, name=name)
-            nc.sync.dma_start(t[:], src)
-            return t
+            dst = lists.tile(list(src.shape), U16, name=name)
+            nc.sync.dma_start(dst[:], src)
+            return dst
 
-        def half_of(lst, a):
-            return lst[:, a * LIST_COLS : (a + 1) * LIST_COLS]
+        def load_row_values(src, name):
+            dst = tile([P, PACK], F32, name)
+            nc.gpsimd.dma_start(dst[:], src.rearrange("(p t) o -> p (t o)", t=PACK))
+            return dst
 
-        def cols(a):
-            return slice(a * HALF, (a + 1) * HALF)
+        def entries(lst, half):
+            return lst[:, half * HALF // GROUP : (half + 1) * HALF // GROUP]
 
-        def gpsimd_copy(dst, src):
-            nc.gpsimd.tensor_scalar(dst, src, 1.0, 0.0, ALU.mult, ALU.add)
+        def places(half):
+            return slice(half * HALF, (half + 1) * HALF)
+
+        def woven(dst, src):
+            return dst.rearrange("p (c i) j -> p c j i", i=RUN), src.rearrange("p j (c i) -> p c j i", i=RUN)
+
+        def quantize(rounded, width, name):
+            codes = tile([P, width], U32, name + "_codes")
+            scales = tile([P, width], U8, name + "_scales")
+            nc.vector.quantize_mx(out=codes[:].bitcast(FP8X4), scales=scales[:], in_=rounded)
+            return codes, scales
+
+        def product(dst, weights, first, codes, scales):
+            w_codes, w_scales = weights
+            nc.tensor.matmul_mx(
+                out=dst[:],
+                lhsT=w_codes[:, first : first + P].bitcast(FP8X4),
+                lhsT_scale=w_scales[:, first : first + P],
+                rhs=codes.bitcast(FP8X4),
+                rhs_scale=scales,
+                start=True,
+                stop=True,
+            )
 
         scale_table = tile([P, T], U8, "scale_table")
         offs_sb = load_list(offs, "offs_sb")
-        scale_rows = x_scales[0].bitcast(I32).unsqueeze(1).to_broadcast([16, 8, T // 4])
+        scale_rows = x_scales[0].bitcast(I32).unsqueeze(1).to_broadcast([P // BLOCK_ROWS, BLOCK_ROWS, T // 4])
         nc.sync.dma_start(scale_table[:].bitcast(I32), scale_rows)
         w1_raw = tile([P, PACK, H], F32, "w1_raw", tag="w_raw")
         nc.sync.dma_start(w1_raw[:], w1.rearrange("(p j) c -> p j c", j=PACK))
@@ -63,202 +90,145 @@ def tile_picked_hasherlratio_none_p_kernel(
         n2_sb = load_list(n2, "n2_sb")
         n3_sb = load_list(n3, "n3_sb")
         n4_sb = load_list(n4, "n4_sb")
-        row_vals = {}
-        for name, src in (("sl", sl), ("th", th), ("gn", gn)):
-            row_vals[name] = tile([P, PACK], F32, name + "_sb")
-            nc.gpsimd.dma_start(row_vals[name][:], src.rearrange("(p t) o -> p (t o)", t=PACK))
-        sl_sb, th_sb, gn_sb = row_vals["sl"], row_vals["th"], row_vals["gn"]
+        sl_sb = load_row_values(sl, "sl_sb")
+        th_sb = load_row_values(th, "th_sb")
+        gn_sb = load_row_values(gn, "gn_sb")
 
         warm_sigmoid = tile([P, 1], F32, "warm_sigmoid")
         nc.scalar.activation(warm_sigmoid[:], w1_raw[:, 0, 0:1], ACT.Sigmoid)
+
         picked_scales = tile([P, S], U8, "picked_scales")
         nc.vector.tensor_copy(picked_scales[:], scale_table[:].indirect(offs_sb[:]))
         x_scale = tile([P, S], U8, "x_scale")
         nc.vector.tensor_copy(x_scale[:].bitcast(I32), picked_scales[:].bitcast(I32))
-        for r in range(1, 4):
-            nc.sync.dma_start(
-                x_scale[:].bitcast(I32)[r:P:32, :], picked_scales[:].bitcast(I32)[8 * r : P : 32, :]
+        for r in range(1, QUADRANT // BLOCK_ROWS):
+            nc.scalar.dma_start(
+                x_scale[:].bitcast(I32)[r:P:QUADRANT, :],
+                picked_scales[:].bitcast(I32)[BLOCK_ROWS * r : P : QUADRANT, :],
             )
 
         w1_bf = tile([P, PACK, P, PACK], BF16, "w1_bf")
-        w1_dst = w1_bf[:].rearrange("p t m j -> p m t j")
-        nc.vector.tensor_copy(w1_dst, w1_raw[:].rearrange("p j (m t) -> p m t j", t=PACK))
-        w1_codes = tile([P, H], U32, "w1_codes")
-        w1_scale = tile([P, H], U8, "w1_scale")
-        nc.vector.quantize_mx(
-            out=w1_codes[:].bitcast(FP8X4), scales=w1_scale[:], in_=w1_bf[:].rearrange("p t m j -> p (t m j)")
+        nc.vector.tensor_copy(
+            w1_bf[:].rearrange("p t m j -> p m t j"), w1_raw[:].rearrange("p j (m t) -> p m t j", t=PACK)
         )
+        w1_mx = quantize(w1_bf[:].rearrange("p t m j -> p (t m j)"), H, "w1")
 
         w2_raw = tile([P, PACK, N], F32, "w2_raw", tag="w_raw")
         nc.sync.dma_start(w2_raw[:], w2.rearrange("(p j) c -> p j c", j=PACK))
 
         y_ps = {}
-        for a in range(2):
-            picked_words = tile([P, HALF], U32, "picked_words%d" % a)
-            nc.vector.tensor_copy(picked_words[:], word_table[:].indirect(half_of(offs_sb, a)))
-            for t in range(PACK):
-                y_ps[t, a] = psum.tile([P, HALF], F32, name="y_ps%d_%d" % (t, a), tag="bank%d" % (4 * a + t))
-                nc.tensor.matmul_mx(
-                    out=y_ps[t, a][:],
-                    lhsT=w1_codes[:, t * P : (t + 1) * P].bitcast(FP8X4),
-                    lhsT_scale=w1_scale[:, t * P : (t + 1) * P],
-                    rhs=picked_words[:].bitcast(FP8X4),
-                    rhs_scale=x_scale[:, cols(a)],
-                    start=True,
-                    stop=True,
-                )
+        for half in HALVES:
+            picked_words = tile([P, HALF], U32, "picked_words%d" % half)
+            nc.vector.tensor_copy(picked_words[:], word_table[:].indirect(entries(offs_sb, half)))
+            for t in TILES:
+                y_ps[t, half] = bank("y_ps", t, half)
+                product(y_ps[t, half], w1_mx, t * P, picked_words[:], x_scale[:, places(half)])
 
         sig_bias = tile([P, PACK], F32, "sig_bias")
         sl_th = tile([P, PACK], F32, "sl_th")
         nc.gpsimd.tensor_tensor(sl_th[:], sl_sb[:], th_sb[:], ALU.mult)
         nc.gpsimd.tensor_scalar(sig_bias[:], sl_th[:], -1.0, 0.0, ALU.mult, ALU.add)
+
+        ds = [tile([P, S], F32, "ds%d" % t) for t in TILES]
         y_sb = {}
-        ds = [tile([P, S], F32, "ds%d" % t) for t in range(PACK)]
-        sg = {}
-        z_planes = {}
 
-        def y_out(t, a):
-            y_sb[t, a] = tile([P, HALF], F32, "y_sb%d_%d" % (t, a))
-            if (t, a) in VEC_OUT:
-                nc.vector.tensor_copy(y_sb[t, a][:], y_ps[t, a][:])
-            else:
-                nc.scalar.copy(y_sb[t, a][:], y_ps[t, a][:])
+        def y_out(t, half):
+            y_sb[t, half] = tile([P, HALF], F32, "y_sb%d_%d" % (t, half))
+            nc.scalar.copy(y_sb[t, half][:], y_ps[t, half][:])
 
-        def y_scatter(t, a):
-            target = ds[t][:].indirect(half_of(n1_sb, a))
-            if t % 2 == 0 or (t, a) == (3, 1):
-                nc.vector.tensor_copy(target, y_sb[t, a][:])
-            else:
-                nc.scalar.activation(target, y_sb[t, a][:], ACT.Copy)
+        def scatter_on_vector(t, half):
+            nc.vector.tensor_copy(ds[t][:].indirect(entries(n1_sb, half)), y_sb[t, half][:])
 
-        def gate(t, a):
-            sg[t, a] = tile([P, HALF], F32, "sg%d_%d" % (t, a))
-            nc.scalar.activation(
-                sg[t, a][:],
-                ds[t][:].indirect(half_of(n2_sb, a)),
-                ACT.Sigmoid,
-                bias=sig_bias[:, t : t + 1],
-                scale=sl_sb[:, t : t + 1],
-            )
+        def scatter_on_scalar(t, half):
+            nc.scalar.activation(ds[t][:].indirect(entries(n1_sb, half)), y_sb[t, half][:], ACT.Copy)
 
-        def z_plane(t, a):
-            if t == 0:
-                z_planes[a] = tile([P, PACK, HALF], BF16, "z_planes%d" % a, tag="planes%d" % a)
-            nc.vector.scalar_tensor_tensor(
-                z_planes[a][:, t, :], y_ps[t, a][:], gn_sb[:, t : t + 1], sg[t, a][:], ALU.mult, ALU.mult
-            )
-
-        w2_bf = {}
-        w2_codes = [tile([P, N // 2], U32, "w2_codes%d" % c) for c in range(2)]
-        w2_scale = [tile([P, N // 2], U8, "w2_scale%d" % c) for c in range(2)]
-
-        def w2_round(c):
-            src = w2_raw[:, :, c * (N // 2) : (c + 1) * (N // 2)]
-            w2_bf[c] = tile([P, N // 2, PACK], BF16, "w2_bf%d" % c, tag="planes%d" % c)
-            gpsimd_copy(w2_bf[c][:].rearrange("p (c i) j -> p c j i", i=4), src.rearrange("p j (c i) -> p c j i", i=4))
-
-        def w2_quantize(c):
-            nc.vector.quantize_mx(
-                out=w2_codes[c][:].bitcast(FP8X4), scales=w2_scale[c][:], in_=w2_bf[c][:].rearrange("p c j -> p (c j)")
-            )
-
-        h_ps = {}
-
-        z_codes, z_scale = {}, {}
-
-        def z_quantize(a):
-            z_bf = tile([P, HALF, PACK], BF16, "z_bf%d" % a)
-            nc.vector.tensor_copy(
-                z_bf[:].rearrange("p (c i) t -> p c t i", i=4), z_planes[a][:].rearrange("p t (c i) -> p c t i", i=4)
-            )
-            z_codes[a] = tile([P, HALF], U32, "z_codes%d" % a)
-            z_scale[a] = tile([P, HALF], U8, "z_scale%d" % a)
-            nc.vector.quantize_mx(
-                out=z_codes[a][:].bitcast(FP8X4), scales=z_scale[a][:], in_=z_bf[:].rearrange("p c t -> p (c t)")
-            )
-
-        def second_product(a, row_tiles):
-            for m in row_tiles:
-                mc = slice((m % 2) * P, (m % 2 + 1) * P)
-                h_ps[m, a] = psum.tile([P, HALF], F32, name="h_ps%d_%d" % (m, a), tag="bank%d" % (4 * a + m))
-                nc.tensor.matmul_mx(
-                    out=h_ps[m, a][:],
-                    lhsT=w2_codes[m // 2][:, mc].bitcast(FP8X4),
-                    lhsT_scale=w2_scale[m // 2][:, mc],
-                    rhs=z_codes[a][:].bitcast(FP8X4),
-                    rhs_scale=z_scale[a][:],
-                    start=True,
-                    stop=True,
-                )
-
-        for t in range(PACK):
+        for t in TILES:
             y_out(t, 0)
         y_out(0, 1)
         y_out(2, 1)
-        y_scatter(0, 0)
-        y_scatter(3, 0)
+        scatter_on_scalar(3, 0)
         y_out(1, 1)
-        y_scatter(2, 0)
-        y_scatter(1, 0)
-        y_scatter(0, 1)
+        scatter_on_scalar(1, 0)
         y_out(3, 1)
-        y_scatter(1, 1)
-        y_scatter(2, 1)
-        y_scatter(3, 1)
-        for c in range(2):
-            w2_round(c)
-        for c in range(2):
-            w2_quantize(c)
-        for t, a in GATES:
-            gate(t, a)
+        scatter_on_scalar(1, 1)
+        for half in HALVES:
+            scatter_on_vector(0, half)
+            scatter_on_vector(2, half)
+        scatter_on_vector(3, 1)
+
+        w2_bf = []
+        for half in HALVES:
+            w2_bf.append(tile([P, N // 2, PACK], BF16, "w2_bf%d" % half, tag="bf16_stage%d" % half))
+            dst, src = woven(w2_bf[half][:], w2_raw[:, :, half * (N // 2) : (half + 1) * (N // 2)])
+            nc.gpsimd.tensor_scalar(dst, src, 1.0, 0.0, ALU.mult, ALU.add)
+        w2_mx = [quantize(w2_bf[half][:].rearrange("p c j -> p (c j)"), N // 2, "w2_%d" % half) for half in HALVES]
+
+        sg = {}
+        for half in HALVES:
+            for t in TILES:
+                sg[t, half] = tile([P, HALF], F32, "sg%d_%d" % (t, half))
+                nc.scalar.activation(
+                    sg[t, half][:],
+                    ds[t][:].indirect(entries(n2_sb, half)),
+                    ACT.Sigmoid,
+                    bias=sig_bias[:, t : t + 1],
+                    scale=sl_sb[:, t : t + 1],
+                )
+
         warm_root = tile([P, 1], F32, "warm_root")
-        nc.scalar.activation(warm_root[:], sg[3, 1][:, 0:1], ACT.Abs_reciprocal_sqrt, bias=0.5)
-        for a in range(2):
-            for t in range(PACK):
-                z_plane(t, a)
-            z_quantize(a)
-            second_product(a, range(PACK))
+        nc.scalar.activation(warm_root[:], sg[PACK - 1, 1][:, 0:1], ACT.Abs_reciprocal_sqrt, bias=0.5)
 
-        pa, pb, rb, inv = {}, {}, {}, {}
-        res = [tile([P, S], F32, "res%d" % m) for m in range(PACK)]
+        h_ps = {}
+        for half in HALVES:
+            z_rows = tile([P, PACK, HALF], BF16, "z_rows%d" % half, tag="bf16_stage%d" % half)
+            for t in TILES:
+                nc.vector.scalar_tensor_tensor(
+                    z_rows[:, t, :], y_ps[t, half][:], gn_sb[:, t : t + 1], sg[t, half][:], ALU.mult, ALU.mult
+                )
+            z_bf = tile([P, HALF, PACK], BF16, "z_bf%d" % half)
+            nc.vector.tensor_copy(*woven(z_bf[:], z_rows[:]))
+            z_codes, z_scales = quantize(z_bf[:].rearrange("p c t -> p (c t)"), HALF, "z%d" % half)
+            for m in TILES:
+                h_ps[m, half] = bank("h_ps", m, half)
+                product(h_ps[m, half], w2_mx[m // 2], (m % 2) * P, z_codes[:], z_scales[:])
 
-        h_all = [tile([P, S], F32, "h_sb%d" % m) for m in range(PACK)]
+        res = [tile([P, S], F32, "res%d" % m) for m in TILES]
+        h_sb = [tile([P, S], F32, "h_sb%d" % m) for m in TILES]
 
-        def h_out(m, a):
-            if (m, a) in VEC_H:
-                nc.vector.tensor_copy(h_all[m][:, cols(a)], h_ps[m, a][:])
-            else:
-                nc.scalar.copy(h_all[m][:, cols(a)], h_ps[m, a][:])
+        for half in HALVES:
+            for m in TILES:
+                if (m, half) == (1, 1):
+                    nc.vector.tensor_copy(h_sb[m][:, places(half)], h_ps[m, half][:])
+                else:
+                    nc.scalar.copy(h_sb[m][:, places(half)], h_ps[m, half][:])
 
-        size, root = {}, {}
+        pa, pb, rb, size, root, inverse = {}, {}, {}, {}, {}, {}
+
+        def pair_tile(kind, name, m):
+            kind[m] = tile([P, W], F32, "%s%d" % (name, m))
+            return kind[m][:]
 
         def fetch(m):
-            pb[m] = tile([P, W], F32, "pb%d" % m)
-            pa[m] = tile([P, W], F32, "pa%d" % m)
-            for i, (dst, lst) in enumerate(((pb[m], n4_sb), (pa[m], n3_sb))):
-                if (m, i) in SC_FETCH:
-                    nc.scalar.activation(dst[:], h_all[m][:].indirect(lst[:]), ACT.Copy)
+            for kind, name, lst in ((pb, "pb", n4_sb), (pa, "pa", n3_sb)):
+                if m == 0:
+                    nc.scalar.activation(pair_tile(kind, name, m), h_sb[m][:].indirect(lst[:]), ACT.Copy)
                 else:
-                    nc.vector.tensor_copy(dst[:], h_all[m][:].indirect(lst[:]))
+                    nc.vector.tensor_copy(pair_tile(kind, name, m), h_sb[m][:].indirect(lst[:]))
 
-        def larger(m):
-            rb[m] = tile([P, W], F32, "rb%d" % m)
-            nc.vector.tensor_tensor(rb[m][:], pa[m][:], pb[m][:], ALU.max)
-
-        def magnitude(m):
-            size[m] = tile([P, W], F32, "size%d" % m)
-            nc.scalar.activation(size[m][:], pb[m][:], ACT.Abs)
-
-        def inverse_root(m):
-            root[m] = tile([P, W], F32, "root%d" % m)
-            nc.scalar.activation(root[m][:], size[m][:], ACT.Abs_reciprocal_sqrt, bias=0.5)
-
-        def inverse(m):
-            inv[m] = tile([P, W], F32, "inv%d" % m)
-            nc.scalar.activation(inv[m][:], root[m][:], ACT.Square)
+        def prepare(row_tiles):
+            for m in row_tiles:
+                fetch(m)
+            for m in row_tiles:
+                nc.vector.tensor_tensor(pair_tile(rb, "rb", m), pa[m][:], pb[m][:], ALU.max)
+            for m in row_tiles:
+                nc.scalar.activation(pair_tile(size, "size", m), pb[m][:], ACT.Abs)
+            for m in row_tiles:
+                nc.scalar.activation(pair_tile(root, "root", m), size[m][:], ACT.Abs_reciprocal_sqrt, bias=0.5)
+            for m in row_tiles:
+                nc.scalar.activation(pair_tile(inverse, "inverse", m), root[m][:], ACT.Square)
 
         def put_ratio(m):
-            nc.vector.tensor_tensor(res[m][:].indirect(n3_sb[:]), pa[m][:], inv[m][:], ALU.mult)
+            nc.vector.tensor_tensor(res[m][:].indirect(n3_sb[:]), pa[m][:], inverse[m][:], ALU.mult)
 
         def put_larger(m):
             nc.scalar.activation(res[m][:].indirect(n4_sb[:]), rb[m][:], ACT.Copy)
@@ -266,21 +236,17 @@ def tile_picked_hasherlratio_none_p_kernel(
         def store(m):
             nc.sync.dma_start(out[m * P : (m + 1) * P, :], res[m][:])
 
-        def prepare(pair):
-            for step in (fetch, larger, magnitude, inverse_root, inverse):
-                for m in pair:
-                    step(m)
-
-        for a in range(2):
-            for m in range(PACK):
-                h_out(m, a)
         prepare((0, 1))
         put_larger(1)
         prepare((2, 3))
-        for m in range(PACK):
-            if m > 0:
-                put_larger((m + 1) % PACK)
-            put_ratio(m)
-            if m > 0:
-                store(m)
+        put_ratio(0)
+        put_ratio(1)
+        store(1)
+        put_larger(3)
+        put_ratio(2)
+        put_larger(0)
         store(0)
+        put_ratio(3)
+        store(3)
+        put_larger(2)
+        store(2)

@@ -102,7 +102,7 @@ def tile_picked_hasherlratio_none_p_kernel(
         x_scale = tile([P, S], U8, "x_scale")
         nc.vector.tensor_copy(x_scale[:].bitcast(I32), picked_scales[:].bitcast(I32))
         for r in range(1, QUADRANT // BLOCK_ROWS):
-            nc.scalar.dma_start(
+            nc.sync.dma_start(
                 x_scale[:].bitcast(I32)[r:P:QUADRANT, :],
                 picked_scales[:].bitcast(I32)[BLOCK_ROWS * r : P : QUADRANT, :],
             )
@@ -159,8 +159,8 @@ def tile_picked_hasherlratio_none_p_kernel(
         w2_bf = []
         for half in HALVES:
             w2_bf.append(tile([P, N // 2, PACK], BF16, "w2_bf%d" % half, tag="bf16_stage%d" % half))
-            dst, src = woven(w2_bf[half][:], w2_raw[:, :, half * (N // 2) : (half + 1) * (N // 2)])
-            nc.gpsimd.tensor_scalar(dst, src, 1.0, 0.0, ALU.mult, ALU.add)
+            src = w2_raw[:, :, half * (N // 2) : (half + 1) * (N // 2)].rearrange("p j c -> p c j")
+            nc.gpsimd.tensor_scalar(w2_bf[half][:], src, 1.0, 0.0, ALU.mult, ALU.add)
         w2_mx = [quantize(w2_bf[half][:].rearrange("p c j -> p (c j)"), N // 2, "w2_%d" % half) for half in HALVES]
 
         sg = {}

from contextlib import ExitStack

import concourse.mybir as mybir

K, T, S, N, H, W = 512, 2048, 512, 512, 512, 256
FLOPS = 2 * K * H * S + 2 * H * N * S

F32 = mybir.dt.float32
BF16 = mybir.dt.bfloat16
I32 = mybir.dt.int32
U32 = mybir.dt.uint32
U16 = mybir.dt.uint16
U8 = mybir.dt.uint8
FP8X4 = mybir.dt.float8_e4m3fn_x4
ALU = mybir.AluOpType
ACT = mybir.ActivationFunctionType

P = 128
PACK = 4
TILES = range(PACK)
HALVES = range(2)
HALF = S // 2
GROUP = 16
BLOCK_ROWS = 8
QUADRANT = 32
RUN = 4


def tile_picked_hasherlratio_none_p_kernel(
    tc, x_words, x_scales, w1, sl, th, gn, w2, offs, n1, n2, n3, n4, out
):
    nc = tc.nc
    with ExitStack() as ctx:
        lists = ctx.enter_context(tc.tile_pool(name="lists", bufs=1))
        sb = ctx.enter_context(tc.tile_pool(name="sb", bufs=1))
        psum = ctx.enter_context(tc.psum_pool(name="psum", bufs=1))

        def tile(shape, dtype, name, tag=None):
            return sb.tile(shape, dtype, name=name, tag=tag or name, align_bytes=64)

        def bank(name, t, half):
            return psum.tile([P, HALF], F32, name="%s%d_%d" % (name, t, half), tag="bank%d" % (PACK * half + t))

        def load_list(src, name):
            dst = lists.tile(list(src.shape), U16, name=name)
            nc.sync.dma_start(dst[:], src)
            return dst

        def load_row_values(src, name):
            dst = tile([P, PACK], F32, name)
            nc.gpsimd.dma_start(dst[:], src.rearrange("(p t) o -> p (t o)", t=PACK))
            return dst

        def entries(lst, half):
            return lst[:, half * HALF // GROUP : (half + 1) * HALF // GROUP]

        def places(half):
            return slice(half * HALF, (half + 1) * HALF)

        def woven(dst, src):
            return dst.rearrange("p (c i) j -> p c j i", i=RUN), src.rearrange("p j (c i) -> p c j i", i=RUN)

        def quantize(rounded, width, name):
            codes = tile([P, width], U32, name + "_codes")
            scales = tile([P, width], U8, name + "_scales")
            nc.vector.quantize_mx(out=codes[:].bitcast(FP8X4), scales=scales[:], in_=rounded)
            return codes, scales

        def product(dst, weights, first, codes, scales):
            w_codes, w_scales = weights
            nc.tensor.matmul_mx(
                out=dst[:],
                lhsT=w_codes[:, first : first + P].bitcast(FP8X4),
                lhsT_scale=w_scales[:, first : first + P],
                rhs=codes.bitcast(FP8X4),
                rhs_scale=scales,
                start=True,
                stop=True,
            )

        scale_table = tile([P, T], U8, "scale_table")
        offs_sb = load_list(offs, "offs_sb")
        scale_rows = x_scales[0].bitcast(I32).unsqueeze(1).to_broadcast([P // BLOCK_ROWS, BLOCK_ROWS, T // 4])
        nc.sync.dma_start(scale_table[:].bitcast(I32), scale_rows)
        w1_raw = tile([P, PACK, H], F32, "w1_raw", tag="w_raw")
        nc.sync.dma_start(w1_raw[:], w1.rearrange("(p j) c -> p j c", j=PACK))
        word_table = tile([P, T], U32, "word_table")
        nc.sync.dma_start(word_table[:].bitcast(I32), x_words[0].rearrange("p c r -> p (c r)").bitcast(I32))
        n1_sb = load_list(n1, "n1_sb")
        n2_sb = load_list(n2, "n2_sb")
        n3_sb = load_list(n3, "n3_sb")
        n4_sb = load_list(n4, "n4_sb")
        sl_sb = load_row_values(sl, "sl_sb")
        th_sb = load_row_values(th, "th_sb")
        gn_sb = load_row_values(gn, "gn_sb")

        warm_sigmoid = tile([P, 1], F32, "warm_sigmoid")
        nc.scalar.activation(warm_sigmoid[:], w1_raw[:, 0, 0:1], ACT.Sigmoid)

        picked_scales = tile([P, S], U8, "picked_scales")
        nc.vector.tensor_copy(picked_scales[:], scale_table[:].indirect(offs_sb[:]))
        x_scale = tile([P, S], U8, "x_scale")
        nc.vector.tensor_copy(x_scale[:].bitcast(I32), picked_scales[:].bitcast(I32))
        for r in range(1, QUADRANT // BLOCK_ROWS):
            nc.sync.dma_start(
                x_scale[:].bitcast(I32)[r:P:QUADRANT, :],
                picked_scales[:].bitcast(I32)[BLOCK_ROWS * r : P : QUADRANT, :],
            )

        w1_bf = tile([P, PACK, P, PACK], BF16, "w1_bf")
        nc.vector.tensor_copy(
            w1_bf[:].rearrange("p t m j -> p m t j"), w1_raw[:].rearrange("p j (m t) -> p m t j", t=PACK)
        )
        w1_mx = quantize(w1_bf[:].rearrange("p t m j -> p (t m j)"), H, "w1")

        w2_raw = tile([P, PACK, N], F32, "w2_raw", tag="w_raw")
        nc.sync.dma_start(w2_raw[:], w2.rearrange("(p j) c -> p j c", j=PACK))

        y_ps = {}
        for half in HALVES:
            picked_words = tile([P, HALF], U32, "picked_words%d" % half)
            nc.vector.tensor_copy(picked_words[:], word_table[:].indirect(entries(offs_sb, half)))
            for t in TILES:
                y_ps[t, half] = bank("y_ps", t, half)
                product(y_ps[t, half], w1_mx, t * P, picked_words[:], x_scale[:, places(half)])

        sig_bias = tile([P, PACK], F32, "sig_bias")
        sl_th = tile([P, PACK], F32, "sl_th")
        nc.gpsimd.tensor_tensor(sl_th[:], sl_sb[:], th_sb[:], ALU.mult)
        nc.gpsimd.tensor_scalar(sig_bias[:], sl_th[:], -1.0, 0.0, ALU.mult, ALU.add)

        ds = [tile([P, S], F32, "ds%d" % t) for t in TILES]
        y_sb = {}

        def y_out(t, half):
            y_sb[t, half] = tile([P, HALF], F32, "y_sb%d_%d" % (t, half))
            nc.scalar.copy(y_sb[t, half][:], y_ps[t, half][:])

        def scatter_on_vector(t, half):
            nc.vector.tensor_copy(ds[t][:].indirect(entries(n1_sb, half)), y_sb[t, half][:])

        def scatter_on_scalar(t, half):
            nc.scalar.activation(ds[t][:].indirect(entries(n1_sb, half)), y_sb[t, half][:], ACT.Copy)

        for t in TILES:
            y_out(t, 0)
        y_out(0, 1)
        y_out(2, 1)
        scatter_on_scalar(3, 0)
        y_out(1, 1)
        scatter_on_scalar(1, 0)
        y_out(3, 1)
        scatter_on_scalar(1, 1)
        for half in HALVES:
            scatter_on_vector(0, half)
            scatter_on_vector(2, half)
        scatter_on_vector(3, 1)

        w2_bf = []
        for half in HALVES:
            w2_bf.append(tile([P, N // 2, PACK], BF16, "w2_bf%d" % half, tag="bf16_stage%d" % half))
            src = w2_raw[:, :, half * (N // 2) : (half + 1) * (N // 2)].rearrange("p j c -> p c j")
            nc.gpsimd.tensor_scalar(w2_bf[half][:], src, 1.0, 0.0, ALU.mult, ALU.add)
        w2_mx = [quantize(w2_bf[half][:].rearrange("p c j -> p (c j)"), N // 2, "w2_%d" % half) for half in HALVES]

        sg = {}
        for half in HALVES:
            for t in TILES:
                sg[t, half] = tile([P, HALF], F32, "sg%d_%d" % (t, half))
                nc.scalar.activation(
                    sg[t, half][:],
                    ds[t][:].indirect(entries(n2_sb, half)),
                    ACT.Sigmoid,
                    bias=sig_bias[:, t : t + 1],
                    scale=sl_sb[:, t : t + 1],
                )

        warm_root = tile([P, 1], F32, "warm_root")
        nc.scalar.activation(warm_root[:], sg[PACK - 1, 1][:, 0:1], ACT.Abs_reciprocal_sqrt, bias=0.5)

        h_ps = {}
        for half in HALVES:
            z_rows = tile([P, PACK, HALF], BF16, "z_rows%d" % half, tag="bf16_stage%d" % half)
            for t in TILES:
                nc.vector.scalar_tensor_tensor(
                    z_rows[:, t, :], y_ps[t, half][:], gn_sb[:, t : t + 1], sg[t, half][:], ALU.mult, ALU.mult
                )
            z_bf = tile([P, HALF, PACK], BF16, "z_bf%d" % half)
            nc.vector.tensor_copy(*woven(z_bf[:], z_rows[:]))
            z_codes, z_scales = quantize(z_bf[:].rearrange("p c t -> p (c t)"), HALF, "z%d" % half)
            for m in TILES:
                h_ps[m, half] = bank("h_ps", m, half)
                product(h_ps[m, half], w2_mx[m // 2], (m % 2) * P, z_codes[:], z_scales[:])

        res = [tile([P, S], F32, "res%d" % m) for m in TILES]
        h_sb = [tile([P, S], F32, "h_sb%d" % m) for m in TILES]

        for half in HALVES:
            for m in TILES:
                if (m, half) == (1, 1):
                    nc.vector.tensor_copy(h_sb[m][:, places(half)], h_ps[m, half][:])
                else:
                    nc.scalar.copy(h_sb[m][:, places(half)], h_ps[m, half][:])

        pa, pb, rb, size, root, inverse = {}, {}, {}, {}, {}, {}

        def pair_tile(kind, name, m):
            kind[m] = tile([P, W], F32, "%s%d" % (name, m))
            return kind[m][:]

        def fetch(m):
            for kind, name, lst in ((pb, "pb", n4_sb), (pa, "pa", n3_sb)):
                if m == 0:
                    nc.scalar.activation(pair_tile(kind, name, m), h_sb[m][:].indirect(lst[:]), ACT.Copy)
                else:
                    nc.vector.tensor_copy(pair_tile(kind, name, m), h_sb[m][:].indirect(lst[:]))

        def prepare(row_tiles):
            for m in row_tiles:
                fetch(m)
            for m in row_tiles:
                nc.vector.tensor_tensor(pair_tile(rb, "rb", m), pa[m][:], pb[m][:], ALU.max)
            for m in row_tiles:
                nc.scalar.activation(pair_tile(size, "size", m), pb[m][:], ACT.Abs)
            for m in row_tiles:
                nc.scalar.activation(pair_tile(root, "root", m), size[m][:], ACT.Abs_reciprocal_sqrt, bias=0.5)
            for m in row_tiles:
                nc.scalar.activation(pair_tile(inverse, "inverse", m), root[m][:], ACT.Square)

        def put_ratio(m):
            nc.vector.tensor_tensor(res[m][:].indirect(n3_sb[:]), pa[m][:], inverse[m][:], ALU.mult)

        def put_larger(m):
            nc.scalar.activation(res[m][:].indirect(n4_sb[:]), rb[m][:], ACT.Copy)

        def store(m):
            nc.sync.dma_start(out[m * P : (m + 1) * P, :], res[m][:])

        prepare((0, 1))
        put_larger(1)
        prepare((2, 3))
        put_ratio(0)
        put_ratio(1)
        store(1)
        put_larger(3)
        put_ratio(2)
        put_larger(0)
        store(0)
        put_ratio(3)
        store(3)
        put_larger(2)
        store(2)
